import numpy as np
import ml_dtypes


def mxq(x, axis, fmt="e4m3"):
    dtype, down = {"e4m3": (ml_dtypes.float8_e4m3fn, 7), "e5m2": (ml_dtypes.float8_e5m2, 14)}[fmt]
    v = np.moveaxis(np.asarray(x, np.float32).astype(ml_dtypes.bfloat16).astype(np.float64), axis, -1)
    blocks = v.reshape(v.shape[:-1] + (-1, 32))
    amax = np.abs(blocks).max(-1, keepdims=True)
    byte = np.maximum(np.where(amax > 0, np.frexp(amax)[1] - 1 + 127, 0) - down, 1)
    scale = np.exp2(byte - 127.0)
    codes = (blocks / scale).astype(np.float32).astype(dtype).astype(np.float64)
    return np.moveaxis((codes * scale).reshape(v.shape), -1, axis)


WIDE = False


def mx_kscale(k):
    if not WIDE:
        return np.ones(k)
    levels = np.array([10, -10, 5, -5, 0])
    if k % 512:
        return np.exp2(np.random.permutation(np.resize(levels, k // 32))).repeat(32)
    a = np.empty((k // 512, 16))
    for p in range(k // 512):
        a[p, :8] = np.random.permutation(np.resize(levels, 8))
        for g in range(8):
            far = levels[np.abs(levels - a[p, g]) >= 10]
            a[p, g + 8] = far[np.random.randint(len(far))]
    return np.exp2(a.ravel()).repeat(32)


def f64(x):
    return np.asarray(x).astype(np.float64)


def striped(idx):
    return np.tile(idx.reshape(-1, 16).T, (8, 1)).astype(np.uint16)


def unstriped(offs):
    return offs[:16].T.reshape(-1).astype(np.int64)


def pack_weight(w):
    k, n = w.shape
    w = f64(np.asarray(w, np.float32).astype(ml_dtypes.bfloat16)).reshape(k // 32, 32, n)
    amax = np.abs(w).max(1)
    byte = np.clip(np.where(amax > 0, np.frexp(amax)[1] - 1 + 127 - 7, 1), 1, 254)
    scaled = (w * np.exp2(127.0 - byte)[:, None, :]).reshape(k, n).astype(np.float32)
    words = np.ascontiguousarray(scaled.reshape(k // 512, 128, 4, n).transpose(0, 1, 3, 2)).astype(ml_dtypes.float8_e4m3fn).view(np.uint8)
    return words, np.ascontiguousarray(byte.astype(np.uint8).reshape(k // 512, 16, n))


def unpack_weight(words, scales):
    g, p, n, _ = words.shape
    vals = np.ascontiguousarray(words).view(ml_dtypes.float8_e4m3fn).astype(np.float64) * np.repeat(np.exp2(scales.astype(np.float64) - 127.0), 8, axis=1)[..., None]
    return vals.transpose(0, 1, 3, 2).reshape(g * 512, n)


def gelu(v):
    return 0.5 * v * (1.0 + np.tanh(np.sqrt(2.0 / np.pi) * (v + 0.044715 * v**3)))


K, T, E, C, N = 512, 4096, 16, 256, 256


def by_expert(wq, xq):
    return np.concatenate([wq[e].T @ xq[:, e * C:(e + 1) * C] for e in range(E)], axis=1)


def setup_inputs():
    n = np.random.standard_normal
    s = mx_kscale(K)[:, None]
    packed = [pack_weight(m) for m in n((E, K, N)) / np.sqrt(K) / s[None]]
    return {
        "xT": (n((K, T)) * s).astype(np.float32),
        "w_words": np.stack([m[0] for m in packed]),
        "w_scales": np.stack([m[1] for m in packed]),
        "b": (0.3 * n((N, E))).astype(np.float32),
        "gate": np.tile(np.random.uniform(0.2, 1.0, E * C), (N, 1)).astype(np.float32),
        "offs": striped(np.random.permutation(T)[:E * C]),
    }


def reference(xT, w_words, w_scales, b, gate, offs):
    idx = unstriped(offs)
    xq = mxq(f64(xT)[:, idx], 0, "e4m3")
    w = np.stack([unpack_weight(w_words[e], w_scales[e]) for e in range(E)])
    y = by_expert(w, xq)
    y = gelu(y + np.repeat(f64(b), C, axis=1))
    out = np.zeros((N, T))
    out[:, idx] = f64(gate) * y
    return out

@@ -1,0 +1,142 @@
+from contextlib import ExitStack
+
+import concourse.mybir as mybir
+
+K, T, E, C, N = 512, 4096, 16, 256, 256
+P = 128
+
+FLOPS = 2 * K * N * E * C
+BYTES = K * T * 4 + E * K * N + E * (K // 32) * N + N * E * 4 + E * C * 4 + P * (E * C // 16) * 2 + N * T * 4
+
+F32 = mybir.dt.float32
+BF16 = mybir.dt.bfloat16
+U32 = mybir.dt.uint32
+I32 = mybir.dt.int32
+U16 = mybir.dt.uint16
+U8 = mybir.dt.uint8
+FP8X4 = mybir.dt.float8_e4m3fn_x4
+ACT = mybir.ActivationFunctionType
+MULT = mybir.AluOpType.mult
+
+HALF = 2048
+QUART = 1024
+
+
+def tile_routed_moe_kernel(tc, xT, w_words, w_scales, b, gate, offs, out):
+    nc = tc.nc
+    with ExitStack() as ctx:
+        held = ctx.enter_context(tc.tile_pool(name="held", bufs=1))
+        stage = ctx.enter_context(tc.tile_pool(name="stage", bufs=5))
+        psum = ctx.enter_context(tc.psum_pool(name="psum", bufs=8))
+
+        offsets = held.tile([P, E * C // 16], U16, name="offsets")
+        nc.sync.dma_start(offsets[:], offs)
+
+        warm = held.tile([P, 1], F32, name="warm")
+        warm_out = held.tile([P, 1], F32, name="warm_out")
+        nc.vector.memset(warm[:], 0.0)
+        nc.scalar.activation(warm_out[:], warm[:], ACT.Gelu_apprx_tanh)
+
+        ws = held.tile([P, E * N], U8, name="ws", align_bytes=64)
+        nc.gpsimd.memset(ws[:].bitcast(I32), 0)
+
+        xv = xT.rearrange("(p u j) n -> u p j n", u=2, j=2)
+        pairs = [held.tile([P, T * 2], BF16, name=f"pairs{u}", align_bytes=64) for u in range(2)]
+        grouped = [held.tile([P, HALF * 4], BF16, name=f"grouped{h}", align_bytes=64) for h in range(2)]
+
+        def load_cast(u, a, width, on_scalar):
+            raw = stage.tile([P, 2, 1024], F32, name="raw")
+            nc.sync.dma_start(raw[:, :, :width], xv[u, :, :, a : a + width])
+            dst = pairs[u][:].rearrange("p (n j) -> p n j", j=2)
+            src = raw[:].rearrange("p j n -> p n j")
+            if on_scalar:
+                nc.scalar.copy(dst[:, a : a + on_scalar, :], src[:, :on_scalar, :])
+            if on_scalar < width:
+                nc.vector.tensor_copy(dst[:, a + on_scalar : a + width, :], src[:, on_scalar:width, :])
+
+        def gather(u, a, width):
+            h, c = divmod(a, HALF)
+            words = grouped[h][:].bitcast(U32).rearrange("p (n u) -> p n u", u=2)
+            nc.vector.tensor_copy(words[:, c : c + width, u], pairs[u][:].bitcast(U32).indirect(offsets[:, a // 16 : (a + width) // 16]))
+
+        for a, width, on_scalar in ((0, 1024, 384), (1024, 1024, 384), (2048, 1024, 384), (3072, 512, 192), (3584, 512, 192)):
+            load_cast(0, a, width, on_scalar)
+        for h in range(2):
+            gather(0, h * HALF, HALF)
+        for a, width, on_scalar in ((0, 1024, 1024), (1024, 1024, 1024), (2048, 1024, 1024), (3072, 512, 256), (3584, 512, 128)):
+            load_cast(1, a, width, on_scalar)
+
+        ww = [held.tile([P, 4 * N], U32, name=f"ww{i}", align_bytes=64) for i in range(4)]
+        for q in range(4):
+            nc.sync.dma_start(
+                ws[32 * q : 32 * q + 4, :].bitcast(I32).rearrange("q (e n) -> q e n", e=E),
+                w_scales[:, 0, 4 * q : 4 * q + 4, :].rearrange("e q n -> q e n").bitcast(I32),
+            )
+        bias = held.tile([P, 2, E], F32, name="bias")
+        nc.sync.dma_start(bias[:], b.rearrange("(h p) e -> p h e", p=P))
+        for i in range(4):
+            nc.sync.dma_start(
+                ww[i][:].bitcast(I32).rearrange("p (e n) -> p e n", e=4),
+                w_words[4 * i : 4 * i + 4, 0].rearrange("e p n r -> p e (n r)").bitcast(I32),
+            )
+        gates = held.tile([P, E * C], F32, name="gates")
+        nc.sync.dma_start(gates[:], gate[0:P, :])
+
+        codes = [held.tile([P, QUART], U32, name=f"codes{c}", align_bytes=64) for c in range(4)]
+        planes = [held.tile([P, QUART], U8, name=f"planes{c}", align_bytes=64) for c in range(4)]
+        ys = [[held.tile([P, HALF], F32, name=f"y{n}{h}") for h in range(2)] for n in range(2)]
+
+        def quantize(c):
+            h, o = divmod(c, 2)
+            nc.vector.quantize_mx(
+                out=codes[c][:].bitcast(FP8X4), scales=planes[c][:], in_=grouped[h][:, o * 4 * QUART : (o + 1) * 4 * QUART]
+            )
+
+        def multiply(c, n):
+            for two in range(2):
+                acc = psum.tile([P, 2 * C], F32, name="acc")
+                for i in range(2):
+                    k = 2 * two + i
+                    e = 4 * c + k
+                    nc.tensor.matmul_mx(
+                        out=acc[:, i * C : (i + 1) * C],
+                        lhsT=ww[c][:, k * N + n * P : k * N + (n + 1) * P].bitcast(FP8X4),
+                        lhsT_scale=ws[:, e * N + n * P : e * N + (n + 1) * P],
+                        rhs=codes[c][:, k * C : (k + 1) * C].bitcast(FP8X4),
+                        rhs_scale=planes[c][:, k * C : (k + 1) * C],
+                        start=True,
+                        stop=True,
+                    )
+                for i in range(2):
+                    e = 4 * c + 2 * two + i
+                    h, o = divmod(e * C, HALF)
+                    nc.scalar.activation(
+                        ys[n][h][:, o : o + C], acc[:, i * C : (i + 1) * C], ACT.Gelu_apprx_tanh, bias=bias[:, n, e : e + 1]
+                    )
+
+        gather(1, 0, QUART)
+        gather(1, QUART, QUART)
+        quantize(0)
+        multiply(0, 0)
+        gather(1, 2 * QUART, QUART)
+        quantize(1)
+        multiply(1, 0)
+        gather(1, 3 * QUART, QUART)
+        quantize(2)
+        multiply(2, 0)
+        quantize(3)
+        multiply(3, 0)
+        for c in range(4):
+            multiply(c, 1)
+
+        for n in range(2):
+            window = held.tile([P, T], F32, name=f"window{n}")
+            for h in range(2):
+                nc.vector.tensor_tensor(
+                    window[:].indirect(offsets[:, h * HALF // 16 : (h + 1) * HALF // 16]),
+                    ys[n][h][:],
+                    gates[:, h * HALF : (h + 1) * HALF],
+                    MULT,
+                )
+            for h in range(2):
+                nc.sync.dma_start(out[n * P : (n + 1) * P, h * HALF : (h + 1) * HALF], window[:, h * HALF : (h + 1) * HALF])

@@ -18,8 +18,9 @@ FP8X4 = mybir.dt.float8_e4m3fn_x4
 ACT = mybir.ActivationFunctionType
 MULT = mybir.AluOpType.mult
 
-HALF = 2048
-QUART = 1024
+CHUNK = 512
+CHUNKS = E * C // CHUNK
+GROUP = 2048
 
 
 def tile_routed_moe_kernel(tc, xT, w_words, w_scales, b, gate, offs, out):
@@ -27,10 +28,9 @@ def tile_routed_moe_kernel(tc, xT, w_words, w_scales, b, gate, offs, out):
     with ExitStack() as ctx:
         held = ctx.enter_context(tc.tile_pool(name="held", bufs=1))
         stage = ctx.enter_context(tc.tile_pool(name="stage", bufs=5))
-        psum = ctx.enter_context(tc.psum_pool(name="psum", bufs=8))
+        psum = ctx.enter_context(tc.psum_pool(name="psum", bufs=4))
 
         offsets = held.tile([P, E * C // 16], U16, name="offsets")
-        nc.sync.dma_start(offsets[:], offs)
 
         warm = held.tile([P, 1], F32, name="warm")
         warm_out = held.tile([P, 1], F32, name="warm_out")
@@ -41,8 +41,9 @@ def tile_routed_moe_kernel(tc, xT, w_words, w_scales, b, gate, offs, out):
         nc.gpsimd.memset(ws[:].bitcast(I32), 0)
 
         xv = xT.rearrange("(p u j) n -> u p j n", u=2, j=2)
-        pairs = [held.tile([P, T * 2], BF16, name=f"pairs{u}", align_bytes=64) for u in range(2)]
-        grouped = [held.tile([P, HALF * 4], BF16, name=f"grouped{h}", align_bytes=64) for h in range(2)]
+        pairs = [held.tile([P, T * 2], BF16, name=f"pairs{u}", tag=f"wide{u}", align_bytes=64) for u in range(2)]
+        planar = [held.tile([P, 2, GROUP], U32, name=f"planar{i}", align_bytes=64) for i in range(2)]
+        grouped = [held.tile([P, CHUNK * 4], BF16, name=f"grouped{c}", align_bytes=64) for c in range(CHUNKS)]
 
         def load_cast(u, a, width, on_scalar):
             raw = stage.tile([P, 2, 1024], F32, name="raw")
@@ -55,15 +56,27 @@ def tile_routed_moe_kernel(tc, xT, w_words, w_scales, b, gate, offs, out):
                 nc.vector.tensor_copy(dst[:, a + on_scalar : a + width, :], src[:, on_scalar:width, :])
 
         def gather(u, a, width):
-            h, c = divmod(a, HALF)
-            words = grouped[h][:].bitcast(U32).rearrange("p (n u) -> p n u", u=2)
-            nc.vector.tensor_copy(words[:, c : c + width, u], pairs[u][:].bitcast(U32).indirect(offsets[:, a // 16 : (a + width) // 16]))
+            i, c = divmod(a, GROUP)
+            nc.vector.tensor_copy(planar[i][:, u, c : c + width], pairs[u][:].bitcast(U32).indirect(offsets[:, a // 16 : (a + width) // 16]))
 
-        for a, width, on_scalar in ((0, 1024, 384), (1024, 1024, 384), (2048, 1024, 384), (3072, 512, 192), (3584, 512, 192)):
+        def interleave(c):
+            i, a = divmod(c * CHUNK, GROUP)
+            words = planar[i][:].rearrange("p u n -> p (u n)").bitcast(BF16).rearrange("p (u n j) -> p n u j", u=2, j=2)
+            if c % 2:
+                nc.scalar.copy(grouped[c][:].rearrange("p (n u j) -> p n u j", u=2, j=2), words[:, a : a + CHUNK, :, :])
+            else:
+                nc.gpsimd.tensor_copy(
+                    grouped[c][:].bitcast(U32).rearrange("p (n u) -> p n u", u=2), planar[i][:, :, a : a + CHUNK].rearrange("p u n -> p n u")
+                )
+
+        load_cast(0, 0, 1024, 320)
+        load_cast(0, 1024, 1024, 320)
+        nc.sync.dma_start(offsets[:], offs)
+        for a, width, on_scalar in ((2048, 1024, 320), (3072, 512, 192), (3584, 512, 192)):
             load_cast(0, a, width, on_scalar)
-        for h in range(2):
-            gather(0, h * HALF, HALF)
-        for a, width, on_scalar in ((0, 1024, 1024), (1024, 1024, 1024), (2048, 1024, 1024), (3072, 512, 256), (3584, 512, 128)):
+        for a in range(0, E * C, GROUP):
+            gather(0, a, GROUP)
+        for a, width, on_scalar in ((0, 1024, 1024), (1024, 1024, 1024), (2048, 1024, 1024), (3072, 512, 512), (3584, 256, 256), (3840, 256, 256)):
             load_cast(1, a, width, on_scalar)
 
         ww = [held.tile([P, 4 * N], U32, name=f"ww{i}", align_bytes=64) for i in range(4)]
@@ -82,61 +95,62 @@ def tile_routed_moe_kernel(tc, xT, w_words, w_scales, b, gate, offs, out):
         gates = held.tile([P, E * C], F32, name="gates")
         nc.sync.dma_start(gates[:], gate[0:P, :])
 
-        codes = [held.tile([P, QUART], U32, name=f"codes{c}", align_bytes=64) for c in range(4)]
-        planes = [held.tile([P, QUART], U8, name=f"planes{c}", align_bytes=64) for c in range(4)]
-        ys = [[held.tile([P, HALF], F32, name=f"y{n}{h}") for h in range(2)] for n in range(2)]
+        codes = [held.tile([P, CHUNK], U32, name=f"codes{c}", align_bytes=64) for c in range(CHUNKS)]
+        planes = [held.tile([P, CHUNK], U8, name=f"planes{c}", align_bytes=64) for c in range(CHUNKS)]
+        cuts = (((0, 1024), (1024, 1024), (2048, 2048)), ((0, 2048), (2048, 2048)))
+        ys = [[held.tile([P, width], F32, name=f"y{n}at{a}") for a, width in cuts[n]] for n in range(2)]
+        windows = [held.tile([P, T], F32, name=f"window{n}", tag=f"wide{n}", align_bytes=64) for n in range(2)]
 
         def quantize(c):
-            h, o = divmod(c, 2)
-            nc.vector.quantize_mx(
-                out=codes[c][:].bitcast(FP8X4), scales=planes[c][:], in_=grouped[h][:, o * 4 * QUART : (o + 1) * 4 * QUART]
-            )
+            nc.vector.quantize_mx(out=codes[c][:].bitcast(FP8X4), scales=planes[c][:], in_=grouped[c][:])
 
         def multiply(c, n):
-            for two in range(2):
-                acc = psum.tile([P, 2 * C], F32, name="acc")
-                for i in range(2):
-                    k = 2 * two + i
-                    e = 4 * c + k
-                    nc.tensor.matmul_mx(
-                        out=acc[:, i * C : (i + 1) * C],
-                        lhsT=ww[c][:, k * N + n * P : k * N + (n + 1) * P].bitcast(FP8X4),
-                        lhsT_scale=ws[:, e * N + n * P : e * N + (n + 1) * P],
-                        rhs=codes[c][:, k * C : (k + 1) * C].bitcast(FP8X4),
-                        rhs_scale=planes[c][:, k * C : (k + 1) * C],
-                        start=True,
-                        stop=True,
-                    )
-                for i in range(2):
-                    e = 4 * c + 2 * two + i
-                    h, o = divmod(e * C, HALF)
-                    nc.scalar.activation(
-                        ys[n][h][:, o : o + C], acc[:, i * C : (i + 1) * C], ACT.Gelu_apprx_tanh, bias=bias[:, n, e : e + 1]
-                    )
-
-        gather(1, 0, QUART)
-        gather(1, QUART, QUART)
-        quantize(0)
-        multiply(0, 0)
-        gather(1, 2 * QUART, QUART)
-        quantize(1)
-        multiply(1, 0)
-        gather(1, 3 * QUART, QUART)
-        quantize(2)
-        multiply(2, 0)
-        quantize(3)
-        multiply(3, 0)
-        for c in range(4):
-            multiply(c, 1)
-
-        for n in range(2):
-            window = held.tile([P, T], F32, name=f"window{n}")
-            for h in range(2):
-                nc.vector.tensor_tensor(
-                    window[:].indirect(offsets[:, h * HALF // 16 : (h + 1) * HALF // 16]),
-                    ys[n][h][:],
-                    gates[:, h * HALF : (h + 1) * HALF],
-                    MULT,
+            acc = psum.tile([P, 2 * C], F32, name=f"acc{n}")
+            for i in range(2):
+                e = 2 * c + i
+                k = e % 4
+                nc.tensor.matmul_mx(
+                    out=acc[:, i * C : (i + 1) * C],
+                    lhsT=ww[e // 4][:, k * N + n * P : k * N + (n + 1) * P].bitcast(FP8X4),
+                    lhsT_scale=ws[:, e * N + n * P : e * N + (n + 1) * P],
+                    rhs=codes[c][:, i * C : (i + 1) * C].bitcast(FP8X4),
+                    rhs_scale=planes[c][:, i * C : (i + 1) * C],
+                    start=True,
+                    stop=True,
                 )
-            for h in range(2):
-                nc.sync.dma_start(out[n * P : (n + 1) * P, h * HALF : (h + 1) * HALF], window[:, h * HALF : (h + 1) * HALF])
+            for i in range(2):
+                e = 2 * c + i
+                for y, (a, width) in zip(ys[n], cuts[n]):
+                    if a <= e * C < a + width:
+                        o = e * C - a
+                        nc.scalar.activation(y[:, o : o + C], acc[:, i * C : (i + 1) * C], ACT.Gelu_apprx_tanh, bias=bias[:, n, e : e + 1])
+
+        def scatter(n, i):
+            a, width = cuts[n][i]
+            nc.vector.tensor_tensor(
+                windows[n][:].indirect(offsets[:, a // 16 : (a + width) // 16]), ys[n][i][:], gates[:, a : a + width], MULT
+            )
+
+        def store(n):
+            queue = (nc.sync, nc.scalar)[n]
+            for a in range(0, T, 2048):
+                queue.dma_start(out[n * P : (n + 1) * P, a : a + 2048], windows[n][:, a : a + 2048])
+
+        def gather_one(i):
+            gather(1, i * 1024, 1024)
+
+        for i in range(4):
+            gather_one(i)
+            interleave(2 * i)
+            interleave(2 * i + 1)
+        for c in range(CHUNKS):
+            quantize(c)
+            multiply(c, 0)
+        for i in range(len(cuts[0])):
+            scatter(0, i)
+        store(0)
+        for c in range(CHUNKS):
+            multiply(c, 1)
+        scatter(1, 0)
+        scatter(1, 1)
+        store(1)

@@ -4,9 +4,28 @@ import concourse.mybir as mybir
 
 K, T, E, C, N = 512, 4096, 16, 256, 256
 P = 128
+SLOTS = E * C
+PAIRS = 2
+LANES = 16
 
-FLOPS = 2 * K * N * E * C
-BYTES = K * T * 4 + E * K * N + E * (K // 32) * N + N * E * 4 + E * C * 4 + P * (E * C // 16) * 2 + N * T * 4
+FIRST_GATHER = 2048
+GROUP = 1024
+BANK = 512
+GROUPS = SLOTS // GROUP
+ON_SCALAR = 512
+
+SCATTERS = (((0, 1024), (1024, 1024), (2048, 2048)), ((0, 2048), (2048, 2048)))
+
+LOADS = (
+    ((0, 1024, 320), (1024, 1024, 320), (2048, 1024, 320), (3072, 512, 160), (3584, 256, 64), (3840, 256, 64)),
+    ((0, 1024, 896), (1024, 1024, 896), (2048, 1024, 896), (3072, 512, 448), (3584, 256, 224), (3840, 256, 224)),
+)
+LOAD_WIDTH = 1024
+STORE_WIDTH = 2048
+WEIGHT_EXPERTS = 4
+
+FLOPS = 2 * K * N * SLOTS
+BYTES = K * T * 4 + E * K * N + E * (K // 32) * N + N * E * 4 + SLOTS * 4 + P * (SLOTS // LANES) * 2 + N * T * 4
 
 F32 = mybir.dt.float32
 BF16 = mybir.dt.bfloat16
@@ -15,12 +34,8 @@ I32 = mybir.dt.int32
 U16 = mybir.dt.uint16
 U8 = mybir.dt.uint8
 FP8X4 = mybir.dt.float8_e4m3fn_x4
-ACT = mybir.ActivationFunctionType
+GELU = mybir.ActivationFunctionType.Gelu_apprx_tanh
 MULT = mybir.AluOpType.mult
-
-CHUNK = 512
-CHUNKS = E * C // CHUNK
-GROUP = 2048
 
 
 def tile_routed_moe_kernel(tc, xT, w_words, w_scales, b, gate, offs, out):
@@ -30,127 +45,132 @@ def tile_routed_moe_kernel(tc, xT, w_words, w_scales, b, gate, offs, out):
         stage = ctx.enter_context(tc.tile_pool(name="stage", bufs=5))
         psum = ctx.enter_context(tc.psum_pool(name="psum", bufs=4))
 
-        offsets = held.tile([P, E * C // 16], U16, name="offsets")
+        offsets = held.tile([P, SLOTS // LANES], U16, name="offsets")
 
-        warm = held.tile([P, 1], F32, name="warm")
-        warm_out = held.tile([P, 1], F32, name="warm_out")
-        nc.vector.memset(warm[:], 0.0)
-        nc.scalar.activation(warm_out[:], warm[:], ACT.Gelu_apprx_tanh)
+        def slots_of_list(first, count):
+            return offsets[:, first // LANES : (first + count) // LANES]
 
-        ws = held.tile([P, E * N], U8, name="ws", align_bytes=64)
-        nc.gpsimd.memset(ws[:].bitcast(I32), 0)
+        zero = held.tile([P, 1], F32, name="zero")
+        gelu_of_zero = held.tile([P, 1], F32, name="gelu_of_zero")
+        nc.vector.memset(zero[:], 0.0)
+        nc.scalar.activation(gelu_of_zero[:], zero[:], GELU)
 
-        xv = xT.rearrange("(p u j) n -> u p j n", u=2, j=2)
-        pairs = [held.tile([P, T * 2], BF16, name=f"pairs{u}", tag=f"wide{u}", align_bytes=64) for u in range(2)]
-        planar = [held.tile([P, 2, GROUP], U32, name=f"planar{i}", align_bytes=64) for i in range(2)]
-        grouped = [held.tile([P, CHUNK * 4], BF16, name=f"grouped{c}", align_bytes=64) for c in range(CHUNKS)]
+        weight_scales = held.tile([P, E * N], U8, name="weight_scales", align_bytes=64)
+        nc.gpsimd.memset(weight_scales[:].bitcast(I32), 0)
 
-        def load_cast(u, a, width, on_scalar):
-            raw = stage.tile([P, 2, 1024], F32, name="raw")
-            nc.sync.dma_start(raw[:, :, :width], xv[u, :, :, a : a + width])
-            dst = pairs[u][:].rearrange("p (n j) -> p n j", j=2)
-            src = raw[:].rearrange("p j n -> p n j")
-            if on_scalar:
-                nc.scalar.copy(dst[:, a : a + on_scalar, :], src[:, :on_scalar, :])
-            if on_scalar < width:
-                nc.vector.tensor_copy(dst[:, a + on_scalar : a + width, :], src[:, on_scalar:width, :])
+        token_words = [held.tile([P, T * 2], BF16, name=f"token_words{u}", tag=f"wide{u}", align_bytes=64) for u in range(PAIRS)]
+        gathered = [held.tile([P, PAIRS, FIRST_GATHER], U32, name=f"gathered{i}", align_bytes=64) for i in range(SLOTS // FIRST_GATHER)]
+        interleaved = [held.tile([P, GROUP * 4], BF16, name=f"interleaved{g}", align_bytes=64) for g in range(GROUPS)]
 
-        def gather(u, a, width):
-            i, c = divmod(a, GROUP)
-            nc.vector.tensor_copy(planar[i][:, u, c : c + width], pairs[u][:].bitcast(U32).indirect(offsets[:, a // 16 : (a + width) // 16]))
+        x_rows = xT.rearrange("(p u j) n -> u p j n", u=PAIRS, j=2)
 
-        def interleave(c):
-            i, a = divmod(c * CHUNK, GROUP)
-            words = planar[i][:].rearrange("p u n -> p (u n)").bitcast(BF16).rearrange("p (u n j) -> p n u j", u=2, j=2)
-            if c % 2:
-                nc.scalar.copy(grouped[c][:].rearrange("p (n u j) -> p n u j", u=2, j=2), words[:, a : a + CHUNK, :, :])
-            else:
-                nc.gpsimd.tensor_copy(
-                    grouped[c][:].bitcast(U32).rearrange("p (n u) -> p n u", u=2), planar[i][:, :, a : a + CHUNK].rearrange("p u n -> p n u")
-                )
+        def load_and_round(u, first, count, on_scalar, other):
+            raw = stage.tile([P, 2, LOAD_WIDTH], F32, name="raw")
+            nc.sync.dma_start(raw[:, :, :count], x_rows[u, :, :, first : first + count])
+            rounded = token_words[u][:].rearrange("p (n j) -> p n j", j=2)
+            values = raw[:].rearrange("p j n -> p n j")
+            nc.scalar.copy(rounded[:, first : first + on_scalar, :], values[:, :on_scalar, :])
+            other.tensor_copy(rounded[:, first + on_scalar : first + count, :], values[:, on_scalar:count, :])
 
-        load_cast(0, 0, 1024, 320)
-        load_cast(0, 1024, 1024, 320)
+        def gather(u, first, count):
+            i, column = divmod(first, FIRST_GATHER)
+            nc.vector.tensor_copy(
+                gathered[i][:, u, column : column + count],
+                token_words[u][:].bitcast(U32).indirect(slots_of_list(first, count)),
+            )
+
+        def interleave(g):
+            i, column = divmod(g * GROUP, FIRST_GATHER)
+            halves = gathered[i][:].rearrange("p u n -> p (u n)").bitcast(BF16).rearrange("p (u n j) -> p n u j", u=PAIRS, j=2)
+            nc.scalar.copy(
+                interleaved[g][:].rearrange("p (n u j) -> p n u j", u=PAIRS, j=2)[:, :ON_SCALAR, :, :],
+                halves[:, column : column + ON_SCALAR, :, :],
+            )
+            nc.gpsimd.tensor_copy(
+                interleaved[g][:].bitcast(U32).rearrange("p (n u) -> p n u", u=PAIRS)[:, ON_SCALAR:, :],
+                gathered[i][:, :, column + ON_SCALAR : column + GROUP].rearrange("p u n -> p n u"),
+            )
+
+        for load in LOADS[0]:
+            load_and_round(0, *load, nc.vector)
         nc.sync.dma_start(offsets[:], offs)
-        for a, width, on_scalar in ((2048, 1024, 320), (3072, 512, 192), (3584, 512, 192)):
-            load_cast(0, a, width, on_scalar)
-        for a in range(0, E * C, GROUP):
-            gather(0, a, GROUP)
-        for a, width, on_scalar in ((0, 1024, 1024), (1024, 1024, 1024), (2048, 1024, 1024), (3072, 512, 512), (3584, 256, 256), (3840, 256, 256)):
-            load_cast(1, a, width, on_scalar)
+        for first in range(0, SLOTS, FIRST_GATHER):
+            gather(0, first, FIRST_GATHER)
+        for load in LOADS[1]:
+            load_and_round(1, *load, nc.gpsimd)
 
-        ww = [held.tile([P, 4 * N], U32, name=f"ww{i}", align_bytes=64) for i in range(4)]
-        for q in range(4):
+        for quadrant in range(4):
             nc.sync.dma_start(
-                ws[32 * q : 32 * q + 4, :].bitcast(I32).rearrange("q (e n) -> q e n", e=E),
-                w_scales[:, 0, 4 * q : 4 * q + 4, :].rearrange("e q n -> q e n").bitcast(I32),
+                weight_scales[32 * quadrant : 32 * quadrant + 4, :].bitcast(I32).rearrange("q (e n) -> q e n", e=E),
+                w_scales[:, 0, 4 * quadrant : 4 * quadrant + 4, :].rearrange("e q n -> q e n").bitcast(I32),
             )
-        bias = held.tile([P, 2, E], F32, name="bias")
-        nc.sync.dma_start(bias[:], b.rearrange("(h p) e -> p h e", p=P))
-        for i in range(4):
+        bias = held.tile([P, N // P, E], F32, name="bias")
+        nc.sync.dma_start(bias[:], b.rearrange("(m p) e -> p m e", p=P))
+        weights = [held.tile([P, WEIGHT_EXPERTS * N], U32, name=f"weights{i}", align_bytes=64) for i in range(E // WEIGHT_EXPERTS)]
+        for i, tile in enumerate(weights):
             nc.sync.dma_start(
-                ww[i][:].bitcast(I32).rearrange("p (e n) -> p e n", e=4),
-                w_words[4 * i : 4 * i + 4, 0].rearrange("e p n r -> p e (n r)").bitcast(I32),
+                tile[:].bitcast(I32).rearrange("p (e n) -> p e n", e=WEIGHT_EXPERTS),
+                w_words[WEIGHT_EXPERTS * i : WEIGHT_EXPERTS * (i + 1), 0].rearrange("e p n r -> p e (n r)").bitcast(I32),
             )
-        gates = held.tile([P, E * C], F32, name="gates")
+        gates = held.tile([P, SLOTS], F32, name="gates")
         nc.sync.dma_start(gates[:], gate[0:P, :])
 
-        codes = [held.tile([P, CHUNK], U32, name=f"codes{c}", align_bytes=64) for c in range(CHUNKS)]
-        planes = [held.tile([P, CHUNK], U8, name=f"planes{c}", align_bytes=64) for c in range(CHUNKS)]
-        cuts = (((0, 1024), (1024, 1024), (2048, 2048)), ((0, 2048), (2048, 2048)))
-        ys = [[held.tile([P, width], F32, name=f"y{n}at{a}") for a, width in cuts[n]] for n in range(2)]
-        windows = [held.tile([P, T], F32, name=f"window{n}", tag=f"wide{n}", align_bytes=64) for n in range(2)]
+        codes = [held.tile([P, GROUP], U32, name=f"codes{g}", align_bytes=64) for g in range(GROUPS)]
+        scales = [held.tile([P, GROUP], U8, name=f"scales{g}", align_bytes=64) for g in range(GROUPS)]
+        results = [[held.tile([P, count], F32, name=f"results{m}at{first}") for first, count in SCATTERS[m]] for m in range(N // P)]
+        windows = [held.tile([P, T], F32, name=f"window{m}", tag=f"wide{m}", align_bytes=64) for m in range(N // P)]
 
-        def quantize(c):
-            nc.vector.quantize_mx(out=codes[c][:].bitcast(FP8X4), scales=planes[c][:], in_=grouped[c][:])
+        def quantize(g):
+            nc.vector.quantize_mx(out=codes[g][:].bitcast(FP8X4), scales=scales[g][:], in_=interleaved[g][:])
 
-        def multiply(c, n):
-            acc = psum.tile([P, 2 * C], F32, name=f"acc{n}")
-            for i in range(2):
-                e = 2 * c + i
-                k = e % 4
-                nc.tensor.matmul_mx(
-                    out=acc[:, i * C : (i + 1) * C],
-                    lhsT=ww[e // 4][:, k * N + n * P : k * N + (n + 1) * P].bitcast(FP8X4),
-                    lhsT_scale=ws[:, e * N + n * P : e * N + (n + 1) * P],
-                    rhs=codes[c][:, i * C : (i + 1) * C].bitcast(FP8X4),
-                    rhs_scale=planes[c][:, i * C : (i + 1) * C],
-                    start=True,
-                    stop=True,
+        def multiply(g, m):
+            for bank_first in range(g * GROUP, (g + 1) * GROUP, BANK):
+                acc = psum.tile([P, BANK], F32, name=f"acc{m}")
+                experts = range(bank_first // C, (bank_first + BANK) // C)
+                for e in experts:
+                    column = e * C - bank_first
+                    slot = e * C - g * GROUP
+                    i, e_in_tile = divmod(e, WEIGHT_EXPERTS)
+                    feature = e_in_tile * N + m * P
+                    nc.tensor.matmul_mx(
+                        out=acc[:, column : column + C],
+                        lhsT=weights[i][:, feature : feature + P].bitcast(FP8X4),
+                        lhsT_scale=weight_scales[:, e * N + m * P : e * N + (m + 1) * P],
+                        rhs=codes[g][:, slot : slot + C].bitcast(FP8X4),
+                        rhs_scale=scales[g][:, slot : slot + C],
+                        start=True,
+                        stop=True,
+                    )
+                for e in experts:
+                    column = e * C - bank_first
+                    for result, (first, count) in zip(results[m], SCATTERS[m]):
+                        if first <= e * C < first + count:
+                            nc.scalar.activation(
+                                result[:, e * C - first : (e + 1) * C - first],
+                                acc[:, column : column + C],
+                                GELU,
+                                bias=bias[:, m, e : e + 1],
+                            )
+
+        def scatter(m):
+            for result, (first, count) in zip(results[m], SCATTERS[m]):
+                nc.vector.tensor_tensor(
+                    windows[m][:].indirect(slots_of_list(first, count)), result[:], gates[:, first : first + count], MULT
                 )
-            for i in range(2):
-                e = 2 * c + i
-                for y, (a, width) in zip(ys[n], cuts[n]):
-                    if a <= e * C < a + width:
-                        o = e * C - a
-                        nc.scalar.activation(y[:, o : o + C], acc[:, i * C : (i + 1) * C], ACT.Gelu_apprx_tanh, bias=bias[:, n, e : e + 1])
 
-        def scatter(n, i):
-            a, width = cuts[n][i]
-            nc.vector.tensor_tensor(
-                windows[n][:].indirect(offsets[:, a // 16 : (a + width) // 16]), ys[n][i][:], gates[:, a : a + width], MULT
-            )
+        def store(m, queue):
+            for first in range(0, T, STORE_WIDTH):
+                queue.dma_start(out[m * P : (m + 1) * P, first : first + STORE_WIDTH], windows[m][:, first : first + STORE_WIDTH])
 
-        def store(n):
-            queue = (nc.sync, nc.scalar)[n]
-            for a in range(0, T, 2048):
-                queue.dma_start(out[n * P : (n + 1) * P, a : a + 2048], windows[n][:, a : a + 2048])
-
-        def gather_one(i):
-            gather(1, i * 1024, 1024)
-
-        for i in range(4):
-            gather_one(i)
-            interleave(2 * i)
-            interleave(2 * i + 1)
-        for c in range(CHUNKS):
-            quantize(c)
-            multiply(c, 0)
-        for i in range(len(cuts[0])):
-            scatter(0, i)
-        store(0)
-        for c in range(CHUNKS):
-            multiply(c, 1)
-        scatter(1, 0)
-        scatter(1, 1)
-        store(1)
+        for g in range(GROUPS):
+            gather(1, g * GROUP, GROUP)
+            interleave(g)
+        for g in range(GROUPS):
+            quantize(g)
+            multiply(g, 0)
+        scatter(0)
+        for g in range(GROUPS):
+            multiply(g, 1)
+        store(0, nc.sync)
+        scatter(1)
+        store(1, nc.scalar)

from contextlib import ExitStack

import concourse.mybir as mybir

K, T, E, C, N = 512, 4096, 16, 256, 256
P = 128
SLOTS = E * C
PAIRS = 2
LANES = 16

FIRST_GATHER = 2048
GROUP = 1024
BANK = 512
GROUPS = SLOTS // GROUP
ON_SCALAR = 512

SCATTERS = (((0, 1024), (1024, 1024), (2048, 2048)), ((0, 2048), (2048, 2048)))

LOADS = (
    ((0, 1024, 320), (1024, 1024, 320), (2048, 1024, 320), (3072, 512, 160), (3584, 256, 64), (3840, 256, 64)),
    ((0, 1024, 896), (1024, 1024, 896), (2048, 1024, 896), (3072, 512, 448), (3584, 256, 224), (3840, 256, 224)),
)
LOAD_WIDTH = 1024
STORE_WIDTH = 2048
WEIGHT_EXPERTS = 4

FLOPS = 2 * K * N * SLOTS
BYTES = K * T * 4 + E * K * N + E * (K // 32) * N + N * E * 4 + SLOTS * 4 + P * (SLOTS // LANES) * 2 + N * T * 4

F32 = mybir.dt.float32
BF16 = mybir.dt.bfloat16
U32 = mybir.dt.uint32
I32 = mybir.dt.int32
U16 = mybir.dt.uint16
U8 = mybir.dt.uint8
FP8X4 = mybir.dt.float8_e4m3fn_x4
GELU = mybir.ActivationFunctionType.Gelu_apprx_tanh
MULT = mybir.AluOpType.mult


def tile_routed_moe_kernel(tc, xT, w_words, w_scales, b, gate, offs, out):
    nc = tc.nc
    with ExitStack() as ctx:
        held = ctx.enter_context(tc.tile_pool(name="held", bufs=1))
        stage = ctx.enter_context(tc.tile_pool(name="stage", bufs=5))
        psum = ctx.enter_context(tc.psum_pool(name="psum", bufs=4))

        offsets = held.tile([P, SLOTS // LANES], U16, name="offsets")

        def slots_of_list(first, count):
            return offsets[:, first // LANES : (first + count) // LANES]

        zero = held.tile([P, 1], F32, name="zero")
        gelu_of_zero = held.tile([P, 1], F32, name="gelu_of_zero")
        nc.vector.memset(zero[:], 0.0)
        nc.scalar.activation(gelu_of_zero[:], zero[:], GELU)

        weight_scales = held.tile([P, E * N], U8, name="weight_scales", align_bytes=64)
        nc.gpsimd.memset(weight_scales[:].bitcast(I32), 0)

        token_words = [held.tile([P, T * 2], BF16, name=f"token_words{u}", tag=f"wide{u}", align_bytes=64) for u in range(PAIRS)]
        gathered = [held.tile([P, PAIRS, FIRST_GATHER], U32, name=f"gathered{i}", align_bytes=64) for i in range(SLOTS // FIRST_GATHER)]
        interleaved = [held.tile([P, GROUP * 4], BF16, name=f"interleaved{g}", align_bytes=64) for g in range(GROUPS)]

        x_rows = xT.rearrange("(p u j) n -> u p j n", u=PAIRS, j=2)

        def load_and_round(u, first, count, on_scalar, other):
            raw = stage.tile([P, 2, LOAD_WIDTH], F32, name="raw")
            nc.sync.dma_start(raw[:, :, :count], x_rows[u, :, :, first : first + count])
            rounded = token_words[u][:].rearrange("p (n j) -> p n j", j=2)
            values = raw[:].rearrange("p j n -> p n j")
            nc.scalar.copy(rounded[:, first : first + on_scalar, :], values[:, :on_scalar, :])
            other.tensor_copy(rounded[:, first + on_scalar : first + count, :], values[:, on_scalar:count, :])

        def gather(u, first, count):
            i, column = divmod(first, FIRST_GATHER)
            nc.vector.tensor_copy(
                gathered[i][:, u, column : column + count],
                token_words[u][:].bitcast(U32).indirect(slots_of_list(first, count)),
            )

        def interleave(g):
            i, column = divmod(g * GROUP, FIRST_GATHER)
            halves = gathered[i][:].rearrange("p u n -> p (u n)").bitcast(BF16).rearrange("p (u n j) -> p n u j", u=PAIRS, j=2)
            nc.scalar.copy(
                interleaved[g][:].rearrange("p (n u j) -> p n u j", u=PAIRS, j=2)[:, :ON_SCALAR, :, :],
                halves[:, column : column + ON_SCALAR, :, :],
            )
            nc.gpsimd.tensor_copy(
                interleaved[g][:].bitcast(U32).rearrange("p (n u) -> p n u", u=PAIRS)[:, ON_SCALAR:, :],
                gathered[i][:, :, column + ON_SCALAR : column + GROUP].rearrange("p u n -> p n u"),
            )

        for load in LOADS[0]:
            load_and_round(0, *load, nc.vector)
        nc.sync.dma_start(offsets[:], offs)
        for first in range(0, SLOTS, FIRST_GATHER):
            gather(0, first, FIRST_GATHER)
        for load in LOADS[1]:
            load_and_round(1, *load, nc.gpsimd)

        for quadrant in range(4):
            nc.sync.dma_start(
                weight_scales[32 * quadrant : 32 * quadrant + 4, :].bitcast(I32).rearrange("q (e n) -> q e n", e=E),
                w_scales[:, 0, 4 * quadrant : 4 * quadrant + 4, :].rearrange("e q n -> q e n").bitcast(I32),
            )
        bias = held.tile([P, N // P, E], F32, name="bias")
        nc.sync.dma_start(bias[:], b.rearrange("(m p) e -> p m e", p=P))
        weights = [held.tile([P, WEIGHT_EXPERTS * N], U32, name=f"weights{i}", align_bytes=64) for i in range(E // WEIGHT_EXPERTS)]
        for i, tile in enumerate(weights):
            nc.sync.dma_start(
                tile[:].bitcast(I32).rearrange("p (e n) -> p e n", e=WEIGHT_EXPERTS),
                w_words[WEIGHT_EXPERTS * i : WEIGHT_EXPERTS * (i + 1), 0].rearrange("e p n r -> p e (n r)").bitcast(I32),
            )
        gates = held.tile([P, SLOTS], F32, name="gates")
        nc.sync.dma_start(gates[:], gate[0:P, :])

        codes = [held.tile([P, GROUP], U32, name=f"codes{g}", align_bytes=64) for g in range(GROUPS)]
        scales = [held.tile([P, GROUP], U8, name=f"scales{g}", align_bytes=64) for g in range(GROUPS)]
        results = [[held.tile([P, count], F32, name=f"results{m}at{first}") for first, count in SCATTERS[m]] for m in range(N // P)]
        windows = [held.tile([P, T], F32, name=f"window{m}", tag=f"wide{m}", align_bytes=64) for m in range(N // P)]

        def quantize(g):
            nc.vector.quantize_mx(out=codes[g][:].bitcast(FP8X4), scales=scales[g][:], in_=interleaved[g][:])

        def multiply(g, m):
            for bank_first in range(g * GROUP, (g + 1) * GROUP, BANK):
                acc = psum.tile([P, BANK], F32, name=f"acc{m}")
                experts = range(bank_first // C, (bank_first + BANK) // C)
                for e in experts:
                    column = e * C - bank_first
                    slot = e * C - g * GROUP
                    i, e_in_tile = divmod(e, WEIGHT_EXPERTS)
                    feature = e_in_tile * N + m * P
                    nc.tensor.matmul_mx(
                        out=acc[:, column : column + C],
                        lhsT=weights[i][:, feature : feature + P].bitcast(FP8X4),
                        lhsT_scale=weight_scales[:, e * N + m * P : e * N + (m + 1) * P],
                        rhs=codes[g][:, slot : slot + C].bitcast(FP8X4),
                        rhs_scale=scales[g][:, slot : slot + C],
                        start=True,
                        stop=True,
                    )
                for e in experts:
                    column = e * C - bank_first
                    for result, (first, count) in zip(results[m], SCATTERS[m]):
                        if first <= e * C < first + count:
                            nc.scalar.activation(
                                result[:, e * C - first : (e + 1) * C - first],
                                acc[:, column : column + C],
                                GELU,
                                bias=bias[:, m, e : e + 1],
                            )

        def scatter(m):
            for result, (first, count) in zip(results[m], SCATTERS[m]):
                nc.vector.tensor_tensor(
                    windows[m][:].indirect(slots_of_list(first, count)), result[:], gates[:, first : first + count], MULT
                )

        def store(m, queue):
            for first in range(0, T, STORE_WIDTH):
                queue.dma_start(out[m * P : (m + 1) * P, first : first + STORE_WIDTH], windows[m][:, first : first + STORE_WIDTH])

        for g in range(GROUPS):
            gather(1, g * GROUP, GROUP)
            interleave(g)
        for g in range(GROUPS):
            quantize(g)
            multiply(g, 0)
        scatter(0)
        for g in range(GROUPS):
            multiply(g, 1)
        store(0, nc.sync)
        scatter(1)
        store(1, nc.scalar)
